import numpy as np
import ml_dtypes


def mxq(x, axis, fmt="e4m3"):
    dtype, down = {"e4m3": (ml_dtypes.float8_e4m3fn, 7), "e5m2": (ml_dtypes.float8_e5m2, 14)}[fmt]
    v = np.moveaxis(np.asarray(x, np.float32).astype(ml_dtypes.bfloat16).astype(np.float64), axis, -1)
    blocks = v.reshape(v.shape[:-1] + (-1, 32))
    amax = np.abs(blocks).max(-1, keepdims=True)
    byte = np.maximum(np.where(amax > 0, np.frexp(amax)[1] - 1 + 127, 0) - down, 1)
    scale = np.exp2(byte - 127.0)
    codes = (blocks / scale).astype(np.float32).astype(dtype).astype(np.float64)
    return np.moveaxis((codes * scale).reshape(v.shape), -1, axis)


WIDE = False


def mx_kscale(k):
    if not WIDE:
        return np.ones(k)
    levels = np.array([10, -10, 5, -5, 0])
    if k % 512:
        return np.exp2(np.random.permutation(np.resize(levels, k // 32))).repeat(32)
    a = np.empty((k // 512, 16))
    for p in range(k // 512):
        a[p, :8] = np.random.permutation(np.resize(levels, 8))
        for g in range(8):
            far = levels[np.abs(levels - a[p, g]) >= 10]
            a[p, g + 8] = far[np.random.randint(len(far))]
    return np.exp2(a.ravel()).repeat(32)


def f64(x):
    return np.asarray(x).astype(np.float64)


def striped(idx):
    return np.tile(idx.reshape(-1, 16).T, (8, 1)).astype(np.uint16)


def unstriped(offs):
    return offs[:16].T.reshape(-1).astype(np.int64)


def pack_weight(w):
    k, n = w.shape
    w = f64(np.asarray(w, np.float32).astype(ml_dtypes.bfloat16)).reshape(k // 32, 32, n)
    amax = np.abs(w).max(1)
    byte = np.clip(np.where(amax > 0, np.frexp(amax)[1] - 1 + 127 - 7, 1), 1, 254)
    scaled = (w * np.exp2(127.0 - byte)[:, None, :]).reshape(k, n).astype(np.float32)
    words = np.ascontiguousarray(scaled.reshape(k // 512, 128, 4, n).transpose(0, 1, 3, 2)).astype(ml_dtypes.float8_e4m3fn).view(np.uint8)
    return words, np.ascontiguousarray(byte.astype(np.uint8).reshape(k // 512, 16, n))


def unpack_weight(words, scales):
    g, p, n, _ = words.shape
    vals = np.ascontiguousarray(words).view(ml_dtypes.float8_e4m3fn).astype(np.float64) * np.repeat(np.exp2(scales.astype(np.float64) - 127.0), 8, axis=1)[..., None]
    return vals.transpose(0, 1, 3, 2).reshape(g * 512, n)


def sigmoid(v):
    return 1.0 / (1.0 + np.exp(-np.maximum(v, -700.0)))


K, T, S, D, N, H, V, U = 512, 2048, 1024, 4, 128, 512, 256, 512


def setup_inputs():
    n = np.random.standard_normal
    s = mx_kscale(K)[:, None]
    u = mx_kscale(H)
    packed_xT = pack_weight(n((K, T)) * s)
    return {
        "x_words": packed_xT[0],
        "x_scales": packed_xT[1],
        "w1": (n((K, H)) / np.sqrt(K) / s).astype(np.float32),
        "amp": (np.random.uniform(0.3, 1.5, (H, U))).astype(np.float32),
        "unit": (np.random.uniform(0.6, 1.4, (H, 1)) * u[:, None]).astype(np.float32),
        "w2": (n((H, N)) / np.sqrt(H) / u[:, None]).astype(np.float32),
        "offs": striped(np.random.permutation(T)[:S]),
        "lag": striped(np.random.permutation(S)),
        "note": striped(np.random.permutation(np.concatenate([np.arange(V), np.random.randint(0, V, U - V)]))),
    }


def reference(x_words, x_scales, w1, amp, unit, w2, offs, lag, note):
    xq = unpack_weight(x_words, x_scales)[:, unstriped(offs)]
    y = mxq(f64(w1), 0, "e4m3").T @ xq
    yl = y[:, unstriped(lag)]
    dfn = (y - yl) ** 2
    cum = dfn.reshape(len(dfn), -1, D).mean(axis=2)
    cmnd = dfn / (np.repeat(cum, D, axis=1) + 0.3)
    best = cmnd.reshape(len(cmnd), -1, D).min(axis=2)
    voi = sigmoid(-3.0 * best + 1.0)
    vn = voi[:, unstriped(note)]
    hid = f64(unit) * (vn * f64(amp) - best[:, unstriped(note)])
    return mxq(f64(w2), 0, "e4m3").T @ mxq(hid, 0, "e4m3")

@@ -1,0 +1,294 @@
+from contextlib import ExitStack
+
+import concourse.mybir as mybir
+from concourse.masks import make_identity
+
+K, T, S, D, N, H, V, U = 512, 2048, 1024, 4, 128, 512, 256, 512
+FLOPS = 2 * K * H * S + 2 * H * N * U
+
+F32 = mybir.dt.float32
+BF16 = mybir.dt.bfloat16
+I32 = mybir.dt.int32
+U32 = mybir.dt.uint32
+U16 = mybir.dt.uint16
+U8 = mybir.dt.uint8
+FP8X4 = mybir.dt.float8_e4m3fn_x4
+ALU = mybir.AluOpType
+ACT = mybir.ActivationFunctionType
+
+P = 128
+PACK = 4
+BANK = 512
+HALVES = S // BANK
+NOTE_HALF = U // 2
+QUARTER = BANK // 2
+GAIN = 5.0
+
+
+def tile_picked_yyinwd_voi_p_kernel(
+    tc, x_words, x_scales, w1, amp, unit, w2, offs, lag, note, out
+):
+    nc = tc.nc
+    with ExitStack() as ctx:
+        keep = ctx.enter_context(tc.tile_pool(name="keep", bufs=1))
+        psum = ctx.enter_context(tc.psum_pool(name="psum", bufs=1))
+
+        offs_t = keep.tile([P, S // 16], U16, name="offs_t")
+        lag_t = keep.tile([P, S // 16], U16, name="lag_t")
+        note_t = keep.tile([P, U // 16], U16, name="note_t")
+        xw = keep.tile([P, T], I32, name="xw", align_bytes=64)
+        xs = keep.tile([P, T], U8, name="xs", align_bytes=64)
+        w1_raw = keep.tile([P, PACK, H], F32, name="w1_raw")
+        w2_raw = keep.tile([P, PACK, N], F32, name="w2_raw")
+        amp_t = keep.tile([P, PACK, U], F32, name="amp_t")
+        unit_t = keep.tile([P, PACK], F32, name="unit_t")
+
+        xs_words = xs[:].bitcast(I32)
+        nc.vector.memset(xs_words[:, 0 : T // 8], 0)
+        nc.gpsimd.memset(xs_words[:, T // 8 : T // 4], 0)
+        nc.sync.dma_start(out=offs_t[:], in_=offs)
+        for q in range(4):
+            queue = nc.scalar if q < 2 else nc.sync
+            queue.dma_start(
+                out=xs[32 * q : 32 * q + 4, :].bitcast(I32),
+                in_=x_scales[0, 4 * q : 4 * q + 4, :].bitcast(I32),
+            )
+        nc.sync.dma_start(out=w1_raw[:], in_=w1.rearrange("(p j) c -> p j c", j=PACK))
+        nc.sync.dma_start(out=xw[:], in_=x_words[0].rearrange("p n t -> p (n t)").bitcast(I32))
+        nc.sync.dma_start(out=lag_t[:], in_=lag)
+        nc.sync.dma_start(out=w2_raw[:], in_=w2.rearrange("(p j) c -> p j c", j=PACK))
+        nc.sync.dma_start(out=unit_t[:], in_=unit.rearrange("(p j) o -> p (j o)", j=PACK))
+        nc.sync.dma_start(out=amp_t[:], in_=amp.rearrange("(p j) c -> p j c", j=PACK))
+        nc.sync.dma_start(out=note_t[:], in_=note)
+        ident = keep.tile([P, P], F32, name="ident")
+        make_identity(nc, ident[:])
+
+        xq_scales = keep.tile([P, S], U8, name="xq_scales", align_bytes=64)
+        nc.vector.tensor_copy(out=xq_scales[:], in_=xs[:].indirect(offs_t[:]))
+
+        w1_view = w1_raw[:].rearrange("p j (m t) -> p m j t", t=PACK)
+        w1_codes, w1_scales = [], []
+        for a in range(2):
+            grouped = keep.tile([P, 2, P, PACK], BF16, name=f"w1_grouped{a}", align_bytes=64)
+            dst = grouped[:].rearrange("p t m j -> p m j t")
+            src = w1_view[:, :, :, 2 * a : 2 * a + 2]
+            if a == 0:
+                nc.vector.tensor_copy(out=dst, in_=src)
+            else:
+                nc.scalar.copy(out=dst, in_=src)
+            for b in range(2):
+                codes = keep.tile([P, P], U32, name=f"w1_codes{a}{b}", align_bytes=64)
+                scales = keep.tile([P, P], U8, name=f"w1_scales{a}{b}", align_bytes=64)
+                nc.vector.quantize_mx(
+                    out=codes[:].bitcast(FP8X4),
+                    scales=scales[:],
+                    in_=grouped[:, b].rearrange("p m j -> p (m j)"),
+                )
+                w1_codes.append(codes)
+                w1_scales.append(scales)
+
+        w2_grouped = keep.tile([P, N, PACK], BF16, name="w2_grouped", align_bytes=64)
+        nc.scalar.copy(
+            out=w2_grouped[:].rearrange("p (c i) j -> p c j i", i=4),
+            in_=w2_raw[:].rearrange("p j (c i) -> p c j i", i=4),
+        )
+
+        xq = [keep.tile([P, BANK], U32, name=f"xq{h}", align_bytes=64) for h in range(HALVES)]
+        for h, lo, hi in ((0, 0, BANK), (1, 0, QUARTER), (1, QUARTER, BANK)):
+            first = h * BANK
+            nc.vector.tensor_copy(
+                out=xq[h][:, lo:hi],
+                in_=xw[:].bitcast(U32).indirect(offs_t[:, (first + lo) // 16 : (first + hi) // 16]),
+            )
+
+        def product(t, h, lo, hi, tag):
+            bank = psum.tile([P, hi - lo], F32, name=f"y_{t}_{h}_{lo}", tag=tag)
+            nc.tensor.matmul_mx(
+                out=bank[:],
+                lhsT=w1_codes[t][:].bitcast(FP8X4),
+                lhsT_scale=w1_scales[t][:],
+                rhs=xq[h][:, lo:hi].bitcast(FP8X4),
+                rhs_scale=xq_scales[:, h * BANK + lo : h * BANK + hi],
+                start=True,
+                stop=True,
+            )
+            return bank
+
+        y = [keep.tile([P, S], F32, name=f"y{t}") for t in range(PACK)]
+        twin = {(t, h): keep.tile([P, BANK], F32, name=f"twin{t}{h}") for t in range(PACK) for h in range(HALVES)}
+        diff = {(t, h): keep.tile([P, BANK], F32, name=f"diff{t}{h}") for t in range(PACK) for h in range(HALVES)}
+        dfn = [keep.tile([P, S], F32, name=f"dfn{t}") for t in range(PACK)]
+        neg_unit = keep.tile([P, PACK], F32, name="neg_unit")
+
+        def half(h):
+            return slice(h * BANK, (h + 1) * BANK)
+
+        def read_out(t, h):
+            nc.scalar.copy(out=y[t][:, half(h)], in_=product(t, h, 0, BANK, f"bank{t}{h}")[:])
+            if t > 0:
+                nc.sync.dma_start(out=twin[t, h][:], in_=y[t][:, half(h)])
+
+        def lagged_difference(t, h):
+            nc.vector.tensor_tensor(
+                out=diff[t, h][:],
+                in0=y[t][:].indirect(lag_t[:, 32 * h : 32 * h + 32]),
+                in1=twin[t, h][:],
+                op=ALU.subtract,
+            )
+
+        def square(t, h):
+            nc.scalar.activation(out=dfn[t][:, half(h)], in_=diff[t, h][:], func=ACT.Square)
+
+        logs = [psum.tile([P, 2 * V], F32, name=f"logs{a}", tag=f"bank{a}1") for a in range(2)]
+
+        def log_denominator(t):
+            sums = psum.tile([P, HALVES, P], F32, name=f"sums{t}", tag=f"bank{t}0")
+            for h in range(HALVES):
+                for d in range(D):
+                    nc.tensor.matmul(
+                        out=sums[:, h, :],
+                        lhsT=dfn[t][:, h * BANK + d : (h + 1) * BANK : D],
+                        rhs=ident[:],
+                        is_transpose=True,
+                        start=(d == 0),
+                        stop=(d == D - 1),
+                    )
+            turned = keep.tile([P, V], F32, name=f"turned{t}", tag="late" if t == PACK - 1 else f"turned{t}")
+            nc.scalar.activation(
+                out=turned[:], in_=sums[:].rearrange("p h i -> p (h i)"), func=ACT.Ln, scale=GAIN / D, bias=0.3 * GAIN - 1.0
+            )
+            for h in range(HALVES):
+                col = (t % 2) * V + h * P
+                nc.tensor.transpose(logs[t // 2][:, col : col + P], turned[:, h * P : (h + 1) * P], ident[:])
+
+        read_out(0, 0)
+        nc.vector.tensor_copy(out=y[0][:, BANK : BANK + QUARTER], in_=product(0, 1, 0, QUARTER, "bank01")[:])
+        nc.vector.tensor_copy(out=twin[0, 0][:], in_=y[0][:, half(0)])
+        read_out(1, 0)
+        nc.vector.tensor_copy(out=y[0][:, BANK + QUARTER : S], in_=product(0, 1, QUARTER, BANK, "bank31")[:])
+        read_out(1, 1)
+        nc.scalar.copy(out=twin[0, 1][:], in_=y[0][:, half(1)])
+        for t in range(PACK):
+            for h in range(HALVES):
+                lagged_difference(t, h)
+            if t + 2 < PACK:
+                for h in range(HALVES):
+                    read_out(t + 2, h)
+            for h in range(HALVES):
+                square(t, h)
+            log_denominator(t)
+
+        recip = []
+        for a in range(2):
+            tile = keep.tile([P, 2 * V], F32, name=f"recip{a}", tag="late" if a == 0 else "recip1")
+            nc.scalar.activation(out=tile[:], in_=logs[a][:], func=ACT.Sigmoid, scale=-1.0)
+            recip.append(tile)
+        for t in range(PACK):
+            scratch = twin[PACK - 1, 1] if t % 2 == 0 else diff[PACK - 1, 0]
+            quads = dfn[t][:].rearrange("p (v a b) -> p v a b", a=2, b=2)
+            pairs = scratch[:].rearrange("p (v b) -> p v b", b=2)
+            nc.vector.tensor_tensor(out=pairs, in0=quads[:, :, 0, :], in1=quads[:, :, 1, :], op=ALU.min)
+            nc.vector.tensor_tensor(out=dfn[t][:, V : 2 * V], in0=pairs[:, :, 0], in1=pairs[:, :, 1], op=ALU.min)
+
+        picked = keep.tile([P, PACK, U], F32, name="picked")
+        voi = keep.tile([P, PACK, U], F32, name="voi")
+        voiced = keep.tile([P, PACK, U], F32, name="voiced")
+        hid = keep.tile([P, PACK, U], BF16, name="hid")
+
+        def best(t):
+            nc.vector.scalar_tensor_tensor(
+                out=dfn[t][:, 0:V],
+                in0=dfn[t][:, V : 2 * V],
+                scalar=GAIN,
+                in1=recip[t // 2][:, (t % 2) * V : (t % 2 + 1) * V],
+                op0=ALU.mult,
+                op1=ALU.mult,
+            )
+
+        def looked_up(t, notes):
+            return dfn[t][:].indirect(note_t[:, notes.start // 16 : notes.stop // 16])
+
+        def voicing(t, notes):
+            nc.scalar.activation(out=voi[:, t, notes], in_=picked[:, t, notes], func=ACT.Sigmoid, scale=-3.0, bias=1.0)
+
+        def pick_and_voice(t, notes):
+            nc.scalar.activation(out=picked[:, t, notes], in_=looked_up(t, notes), func=ACT.Copy)
+            voicing(t, notes)
+
+        def amplitude(t, notes):
+            nc.vector.scalar_tensor_tensor(
+                out=voiced[:, t, notes],
+                in0=voi[:, t, notes],
+                scalar=unit_t[:, t : t + 1],
+                in1=amp_t[:, t, notes],
+                op0=ALU.mult,
+                op1=ALU.mult,
+            )
+
+        def hidden(t, notes):
+            nc.vector.scalar_tensor_tensor(
+                out=hid[:, t, notes],
+                in0=picked[:, t, notes],
+                scalar=neg_unit[:, t : t + 1],
+                in1=voiced[:, t, notes],
+                op0=ALU.mult,
+                op1=ALU.add,
+            )
+
+        nc.vector.tensor_scalar(out=neg_unit[:], in0=unit_t[:], scalar1=-1.0, scalar2=None, op0=ALU.mult)
+        w2_codes = keep.tile([P, N], U32, name="w2_codes", align_bytes=64)
+        w2_scales = keep.tile([P, N], U8, name="w2_scales", align_bytes=64)
+        nc.vector.quantize_mx(
+            out=w2_codes[:].bitcast(FP8X4), scales=w2_scales[:], in_=w2_grouped[:].rearrange("p c j -> p (c j)")
+        )
+
+        every = slice(0, U)
+        early, late = slice(0, NOTE_HALF), slice(NOTE_HALF, U)
+        for t in range(3):
+            best(t)
+        pick_and_voice(0, every)
+        nc.vector.tensor_copy(out=picked[:, 1, :], in_=looked_up(1, every))
+        best(3)
+        voicing(1, every)
+        pick_and_voice(2, every)
+        pick_and_voice(3, early)
+        pick_and_voice(3, late)
+        for steps in (((0, every), (1, every)), ((2, every), (3, early)), ((3, late),)):
+            for t, notes in steps:
+                amplitude(t, notes)
+            for t, notes in steps:
+                hidden(t, notes)
+
+        grouped = []
+        for h, notes in enumerate((early, late)):
+            tile = keep.tile([P, NOTE_HALF, PACK], BF16, name=f"hid_grouped{h}", align_bytes=64)
+            dst = tile[:].rearrange("p (c i) t -> p c t i", i=4)
+            src = hid[:, :, notes].rearrange("p t (c i) -> p c t i", i=4)
+            if h == 0:
+                nc.scalar.copy(out=dst, in_=src)
+            else:
+                nc.vector.tensor_copy(out=dst, in_=src)
+            grouped.append(tile)
+        for h, notes in ((1, late), (0, early)):
+            codes = keep.tile([P, NOTE_HALF], U32, name=f"hid_codes{h}", align_bytes=64)
+            scales = keep.tile([P, NOTE_HALF], U8, name=f"hid_scales{h}", align_bytes=64)
+            nc.vector.quantize_mx(
+                out=codes[:].bitcast(FP8X4), scales=scales[:], in_=grouped[h][:].rearrange("p c t -> p (c t)")
+            )
+            acc = psum.tile([P, NOTE_HALF], F32, name=f"acc{h}", tag=f"bank{h}0")
+            nc.tensor.matmul_mx(
+                out=acc[:],
+                lhsT=w2_codes[:].bitcast(FP8X4),
+                lhsT_scale=w2_scales[:],
+                rhs=codes[:].bitcast(FP8X4),
+                rhs_scale=scales[:],
+                start=True,
+                stop=True,
+            )
+            result = keep.tile([P, NOTE_HALF], F32, name=f"result{h}")
+            if h == 1:
+                nc.scalar.copy(out=result[:], in_=acc[:])
+                nc.scalar.dma_start(out=out[:, notes], in_=result[:])
+            else:
+                nc.vector.tensor_copy(out=result[:], in_=acc[:])
+                nc.sync.dma_start(out=out[:, notes], in_=result[:])

@@ -87,12 +87,6 @@ def tile_picked_yyinwd_voi_p_kernel(
                 w1_codes.append(codes)
                 w1_scales.append(scales)
 
-        w2_grouped = keep.tile([P, N, PACK], BF16, name="w2_grouped", align_bytes=64)
-        nc.scalar.copy(
-            out=w2_grouped[:].rearrange("p (c i) j -> p c j i", i=4),
-            in_=w2_raw[:].rearrange("p j (c i) -> p c j i", i=4),
-        )
-
         xq = [keep.tile([P, BANK], U32, name=f"xq{h}", align_bytes=64) for h in range(HALVES)]
         for h, lo, hi in ((0, 0, BANK), (1, 0, QUARTER), (1, QUARTER, BANK)):
             first = h * BANK
@@ -115,10 +109,9 @@ def tile_picked_yyinwd_voi_p_kernel(
             return bank
 
         y = [keep.tile([P, S], F32, name=f"y{t}") for t in range(PACK)]
-        twin = {(t, h): keep.tile([P, BANK], F32, name=f"twin{t}{h}") for t in range(PACK) for h in range(HALVES)}
+        twin = {(t, h): keep.tile([P, BANK], F32, name=f"twin{t}{h}", tag=f"twin{t}{h}", align_bytes=64) for t in range(PACK) for h in range(HALVES)}
         diff = {(t, h): keep.tile([P, BANK], F32, name=f"diff{t}{h}") for t in range(PACK) for h in range(HALVES)}
         dfn = [keep.tile([P, S], F32, name=f"dfn{t}") for t in range(PACK)]
-        neg_unit = keep.tile([P, PACK], F32, name="neg_unit")
 
         def half(h):
             return slice(h * BANK, (h + 1) * BANK)
@@ -128,16 +121,21 @@ def tile_picked_yyinwd_voi_p_kernel(
             if t > 0:
                 nc.sync.dma_start(out=twin[t, h][:], in_=y[t][:, half(h)])
 
-        def lagged_difference(t, h):
+        def lagged_difference(t, h, lo, hi):
+            first = h * BANK
             nc.vector.tensor_tensor(
-                out=diff[t, h][:],
-                in0=y[t][:].indirect(lag_t[:, 32 * h : 32 * h + 32]),
-                in1=twin[t, h][:],
+                out=diff[t, h][:, lo:hi],
+                in0=y[t][:].indirect(lag_t[:, (first + lo) // 16 : (first + hi) // 16]),
+                in1=twin[t, h][:, lo:hi],
                 op=ALU.subtract,
             )
 
-        def square(t, h):
-            nc.scalar.activation(out=dfn[t][:, half(h)], in_=diff[t, h][:], func=ACT.Square)
+        def square(t, h, lo, hi):
+            nc.scalar.activation(
+                out=dfn[t][:, half(h)].rearrange("p (d v) -> p v d", d=D)[:, lo // D : hi // D, :],
+                in_=diff[t, h][:, lo:hi].rearrange("p (v d) -> p v d", d=D),
+                func=ACT.Square,
+            )
 
         logs = [psum.tile([P, 2 * V], F32, name=f"logs{a}", tag=f"bank{a}1") for a in range(2)]
 
@@ -147,7 +145,7 @@ def tile_picked_yyinwd_voi_p_kernel(
                 for d in range(D):
                     nc.tensor.matmul(
                         out=sums[:, h, :],
-                        lhsT=dfn[t][:, h * BANK + d : (h + 1) * BANK : D],
+                        lhsT=dfn[t][:, h * BANK + d * P : h * BANK + (d + 1) * P],
                         rhs=ident[:],
                         is_transpose=True,
                         start=(d == 0),
@@ -162,20 +160,21 @@ def tile_picked_yyinwd_voi_p_kernel(
                 nc.tensor.transpose(logs[t // 2][:, col : col + P], turned[:, h * P : (h + 1) * P], ident[:])
 
         read_out(0, 0)
-        nc.vector.tensor_copy(out=y[0][:, BANK : BANK + QUARTER], in_=product(0, 1, 0, QUARTER, "bank01")[:])
+        nc.vector.tensor_copy(out=y[0][:, BANK : BANK + QUARTER], in_=product(0, 1, 0, QUARTER, "bank20")[:])
         nc.vector.tensor_copy(out=twin[0, 0][:], in_=y[0][:, half(0)])
         read_out(1, 0)
-        nc.vector.tensor_copy(out=y[0][:, BANK + QUARTER : S], in_=product(0, 1, QUARTER, BANK, "bank31")[:])
-        read_out(1, 1)
+        nc.vector.tensor_copy(out=y[0][:, BANK + QUARTER : S], in_=product(0, 1, QUARTER, BANK, "bank30")[:])
         nc.scalar.copy(out=twin[0, 1][:], in_=y[0][:, half(1)])
+        read_out(1, 1)
+        for t in range(2, PACK):
+            for h in range(HALVES):
+                read_out(t, h)
         for t in range(PACK):
-            for h in range(HALVES):
-                lagged_difference(t, h)
-            if t + 2 < PACK:
-                for h in range(HALVES):
-                    read_out(t + 2, h)
-            for h in range(HALVES):
-                square(t, h)
+            pieces = [(0, 0, BANK), (1, 0, BANK)] if t < PACK - 1 else [(0, 0, BANK), (1, 0, QUARTER), (1, QUARTER, BANK)]
+            for piece in pieces:
+                lagged_difference(t, *piece)
+            for piece in pieces:
+                square(t, *piece)
             log_denominator(t)
 
         recip = []
@@ -185,10 +184,14 @@ def tile_picked_yyinwd_voi_p_kernel(
             recip.append(tile)
         for t in range(PACK):
             scratch = twin[PACK - 1, 1] if t % 2 == 0 else diff[PACK - 1, 0]
-            quads = dfn[t][:].rearrange("p (v a b) -> p v a b", a=2, b=2)
-            pairs = scratch[:].rearrange("p (v b) -> p v b", b=2)
-            nc.vector.tensor_tensor(out=pairs, in0=quads[:, :, 0, :], in1=quads[:, :, 1, :], op=ALU.min)
-            nc.vector.tensor_tensor(out=dfn[t][:, V : 2 * V], in0=pairs[:, :, 0], in1=pairs[:, :, 1], op=ALU.min)
+            planes = dfn[t][:].rearrange("p (h a c) -> p h a c", h=HALVES, a=2)
+            nc.vector.tensor_tensor(
+                out=scratch[:].rearrange("p (h c) -> p h c", h=HALVES), in0=planes[:, :, 0, :], in1=planes[:, :, 1, :], op=ALU.min
+            )
+            pairs = scratch[:].rearrange("p (h b v) -> p h b v", h=HALVES, b=2)
+            nc.vector.tensor_tensor(
+                out=dfn[t][:, V : 2 * V].rearrange("p (h v) -> p h v", h=HALVES), in0=pairs[:, :, 0, :], in1=pairs[:, :, 1, :], op=ALU.min
+            )
 
         picked = keep.tile([P, PACK, U], F32, name="picked")
         voi = keep.tile([P, PACK, U], F32, name="voi")
@@ -199,7 +202,7 @@ def tile_picked_yyinwd_voi_p_kernel(
             nc.vector.scalar_tensor_tensor(
                 out=dfn[t][:, 0:V],
                 in0=dfn[t][:, V : 2 * V],
-                scalar=GAIN,
+                scalar=-GAIN,
                 in1=recip[t // 2][:, (t % 2) * V : (t % 2 + 1) * V],
                 op0=ALU.mult,
                 op1=ALU.mult,
@@ -209,7 +212,7 @@ def tile_picked_yyinwd_voi_p_kernel(
             return dfn[t][:].indirect(note_t[:, notes.start // 16 : notes.stop // 16])
 
         def voicing(t, notes):
-            nc.scalar.activation(out=voi[:, t, notes], in_=picked[:, t, notes], func=ACT.Sigmoid, scale=-3.0, bias=1.0)
+            nc.scalar.activation(out=voi[:, t, notes], in_=picked[:, t, notes], func=ACT.Sigmoid, scale=3.0, bias=1.0)
 
         def pick_and_voice(t, notes):
             nc.scalar.activation(out=picked[:, t, notes], in_=looked_up(t, notes), func=ACT.Copy)
@@ -229,13 +232,17 @@ def tile_picked_yyinwd_voi_p_kernel(
             nc.vector.scalar_tensor_tensor(
                 out=hid[:, t, notes],
                 in0=picked[:, t, notes],
-                scalar=neg_unit[:, t : t + 1],
+                scalar=unit_t[:, t : t + 1],
                 in1=voiced[:, t, notes],
                 op0=ALU.mult,
                 op1=ALU.add,
             )
 
-        nc.vector.tensor_scalar(out=neg_unit[:], in0=unit_t[:], scalar1=-1.0, scalar2=None, op0=ALU.mult)
+        w2_grouped = keep.tile([P, N, PACK], BF16, name="w2_grouped", tag="twin30", align_bytes=64)
+        nc.vector.tensor_copy(
+            out=w2_grouped[:].rearrange("p (c i) j -> p c j i", i=4),
+            in_=w2_raw[:].rearrange("p j (c i) -> p c j i", i=4),
+        )
         w2_codes = keep.tile([P, N], U32, name="w2_codes", align_bytes=64)
         w2_scales = keep.tile([P, N], U8, name="w2_scales", align_bytes=64)
         nc.vector.quantize_mx(

@@ -62,6 +62,8 @@ def tile_picked_yyinwd_voi_p_kernel(
         nc.sync.dma_start(out=note_t[:], in_=note)
         ident = keep.tile([P, P], F32, name="ident")
         make_identity(nc, ident[:])
+        warm = keep.tile([P, 1], F32, name="warm")
+        nc.scalar.activation(out=warm[:], in_=ident[:, 0:1], func=ACT.Ln, scale=GAIN / D, bias=0.3 * GAIN - 1.0)
 
         xq_scales = keep.tile([P, S], U8, name="xq_scales", align_bytes=64)
         nc.vector.tensor_copy(out=xq_scales[:], in_=xs[:].indirect(offs_t[:]))

from contextlib import ExitStack

import concourse.mybir as mybir
from concourse.masks import make_identity

K, T, S, D, N, H, V, U = 512, 2048, 1024, 4, 128, 512, 256, 512
FLOPS = 2 * K * H * S + 2 * H * N * U

F32 = mybir.dt.float32
BF16 = mybir.dt.bfloat16
I32 = mybir.dt.int32
U32 = mybir.dt.uint32
U16 = mybir.dt.uint16
U8 = mybir.dt.uint8
FP8X4 = mybir.dt.float8_e4m3fn_x4
ALU = mybir.AluOpType
ACT = mybir.ActivationFunctionType

P = 128
PACK = 4
BANK = 512
HALVES = S // BANK
NOTE_HALF = U // 2
QUARTER = BANK // 2
GAIN = 5.0


def tile_picked_yyinwd_voi_p_kernel(
    tc, x_words, x_scales, w1, amp, unit, w2, offs, lag, note, out
):
    nc = tc.nc
    with ExitStack() as ctx:
        keep = ctx.enter_context(tc.tile_pool(name="keep", bufs=1))
        psum = ctx.enter_context(tc.psum_pool(name="psum", bufs=1))

        offs_t = keep.tile([P, S // 16], U16, name="offs_t")
        lag_t = keep.tile([P, S // 16], U16, name="lag_t")
        note_t = keep.tile([P, U // 16], U16, name="note_t")
        xw = keep.tile([P, T], I32, name="xw", align_bytes=64)
        xs = keep.tile([P, T], U8, name="xs", align_bytes=64)
        w1_raw = keep.tile([P, PACK, H], F32, name="w1_raw")
        w2_raw = keep.tile([P, PACK, N], F32, name="w2_raw")
        amp_t = keep.tile([P, PACK, U], F32, name="amp_t")
        unit_t = keep.tile([P, PACK], F32, name="unit_t")

        xs_words = xs[:].bitcast(I32)
        nc.vector.memset(xs_words[:, 0 : T // 8], 0)
        nc.gpsimd.memset(xs_words[:, T // 8 : T // 4], 0)
        nc.sync.dma_start(out=offs_t[:], in_=offs)
        for q in range(4):
            queue = nc.scalar if q < 2 else nc.sync
            queue.dma_start(
                out=xs[32 * q : 32 * q + 4, :].bitcast(I32),
                in_=x_scales[0, 4 * q : 4 * q + 4, :].bitcast(I32),
            )
        nc.sync.dma_start(out=w1_raw[:], in_=w1.rearrange("(p j) c -> p j c", j=PACK))
        nc.sync.dma_start(out=xw[:], in_=x_words[0].rearrange("p n t -> p (n t)").bitcast(I32))
        nc.sync.dma_start(out=lag_t[:], in_=lag)
        nc.sync.dma_start(out=w2_raw[:], in_=w2.rearrange("(p j) c -> p j c", j=PACK))
        nc.sync.dma_start(out=unit_t[:], in_=unit.rearrange("(p j) o -> p (j o)", j=PACK))
        nc.sync.dma_start(out=amp_t[:], in_=amp.rearrange("(p j) c -> p j c", j=PACK))
        nc.sync.dma_start(out=note_t[:], in_=note)
        ident = keep.tile([P, P], F32, name="ident")
        make_identity(nc, ident[:])
        warm = keep.tile([P, 1], F32, name="warm")
        nc.scalar.activation(out=warm[:], in_=ident[:, 0:1], func=ACT.Ln, scale=GAIN / D, bias=0.3 * GAIN - 1.0)

        xq_scales = keep.tile([P, S], U8, name="xq_scales", align_bytes=64)
        nc.vector.tensor_copy(out=xq_scales[:], in_=xs[:].indirect(offs_t[:]))

        w1_view = w1_raw[:].rearrange("p j (m t) -> p m j t", t=PACK)
        w1_codes, w1_scales = [], []
        for a in range(2):
            grouped = keep.tile([P, 2, P, PACK], BF16, name=f"w1_grouped{a}", align_bytes=64)
            dst = grouped[:].rearrange("p t m j -> p m j t")
            src = w1_view[:, :, :, 2 * a : 2 * a + 2]
            if a == 0:
                nc.vector.tensor_copy(out=dst, in_=src)
            else:
                nc.scalar.copy(out=dst, in_=src)
            for b in range(2):
                codes = keep.tile([P, P], U32, name=f"w1_codes{a}{b}", align_bytes=64)
                scales = keep.tile([P, P], U8, name=f"w1_scales{a}{b}", align_bytes=64)
                nc.vector.quantize_mx(
                    out=codes[:].bitcast(FP8X4),
                    scales=scales[:],
                    in_=grouped[:, b].rearrange("p m j -> p (m j)"),
                )
                w1_codes.append(codes)
                w1_scales.append(scales)

        xq = [keep.tile([P, BANK], U32, name=f"xq{h}", align_bytes=64) for h in range(HALVES)]
        for h, lo, hi in ((0, 0, BANK), (1, 0, QUARTER), (1, QUARTER, BANK)):
            first = h * BANK
            nc.vector.tensor_copy(
                out=xq[h][:, lo:hi],
                in_=xw[:].bitcast(U32).indirect(offs_t[:, (first + lo) // 16 : (first + hi) // 16]),
            )

        def product(t, h, lo, hi, tag):
            bank = psum.tile([P, hi - lo], F32, name=f"y_{t}_{h}_{lo}", tag=tag)
            nc.tensor.matmul_mx(
                out=bank[:],
                lhsT=w1_codes[t][:].bitcast(FP8X4),
                lhsT_scale=w1_scales[t][:],
                rhs=xq[h][:, lo:hi].bitcast(FP8X4),
                rhs_scale=xq_scales[:, h * BANK + lo : h * BANK + hi],
                start=True,
                stop=True,
            )
            return bank

        y = [keep.tile([P, S], F32, name=f"y{t}") for t in range(PACK)]
        twin = {(t, h): keep.tile([P, BANK], F32, name=f"twin{t}{h}", tag=f"twin{t}{h}", align_bytes=64) for t in range(PACK) for h in range(HALVES)}
        diff = {(t, h): keep.tile([P, BANK], F32, name=f"diff{t}{h}") for t in range(PACK) for h in range(HALVES)}
        dfn = [keep.tile([P, S], F32, name=f"dfn{t}") for t in range(PACK)]

        def half(h):
            return slice(h * BANK, (h + 1) * BANK)

        def read_out(t, h):
            nc.scalar.copy(out=y[t][:, half(h)], in_=product(t, h, 0, BANK, f"bank{t}{h}")[:])
            if t > 0:
                nc.sync.dma_start(out=twin[t, h][:], in_=y[t][:, half(h)])

        def lagged_difference(t, h, lo, hi):
            first = h * BANK
            nc.vector.tensor_tensor(
                out=diff[t, h][:, lo:hi],
                in0=y[t][:].indirect(lag_t[:, (first + lo) // 16 : (first + hi) // 16]),
                in1=twin[t, h][:, lo:hi],
                op=ALU.subtract,
            )

        def square(t, h, lo, hi):
            nc.scalar.activation(
                out=dfn[t][:, half(h)].rearrange("p (d v) -> p v d", d=D)[:, lo // D : hi // D, :],
                in_=diff[t, h][:, lo:hi].rearrange("p (v d) -> p v d", d=D),
                func=ACT.Square,
            )

        logs = [psum.tile([P, 2 * V], F32, name=f"logs{a}", tag=f"bank{a}1") for a in range(2)]

        def log_denominator(t):
            sums = psum.tile([P, HALVES, P], F32, name=f"sums{t}", tag=f"bank{t}0")
            for h in range(HALVES):
                for d in range(D):
                    nc.tensor.matmul(
                        out=sums[:, h, :],
                        lhsT=dfn[t][:, h * BANK + d * P : h * BANK + (d + 1) * P],
                        rhs=ident[:],
                        is_transpose=True,
                        start=(d == 0),
                        stop=(d == D - 1),
                    )
            turned = keep.tile([P, V], F32, name=f"turned{t}", tag="late" if t == PACK - 1 else f"turned{t}")
            nc.scalar.activation(
                out=turned[:], in_=sums[:].rearrange("p h i -> p (h i)"), func=ACT.Ln, scale=GAIN / D, bias=0.3 * GAIN - 1.0
            )
            for h in range(HALVES):
                col = (t % 2) * V + h * P
                nc.tensor.transpose(logs[t // 2][:, col : col + P], turned[:, h * P : (h + 1) * P], ident[:])

        read_out(0, 0)
        nc.vector.tensor_copy(out=y[0][:, BANK : BANK + QUARTER], in_=product(0, 1, 0, QUARTER, "bank20")[:])
        nc.vector.tensor_copy(out=twin[0, 0][:], in_=y[0][:, half(0)])
        read_out(1, 0)
        nc.vector.tensor_copy(out=y[0][:, BANK + QUARTER : S], in_=product(0, 1, QUARTER, BANK, "bank30")[:])
        nc.scalar.copy(out=twin[0, 1][:], in_=y[0][:, half(1)])
        read_out(1, 1)
        for t in range(2, PACK):
            for h in range(HALVES):
                read_out(t, h)
        for t in range(PACK):
            pieces = [(0, 0, BANK), (1, 0, BANK)] if t < PACK - 1 else [(0, 0, BANK), (1, 0, QUARTER), (1, QUARTER, BANK)]
            for piece in pieces:
                lagged_difference(t, *piece)
            for piece in pieces:
                square(t, *piece)
            log_denominator(t)

        recip = []
        for a in range(2):
            tile = keep.tile([P, 2 * V], F32, name=f"recip{a}", tag="late" if a == 0 else "recip1")
            nc.scalar.activation(out=tile[:], in_=logs[a][:], func=ACT.Sigmoid, scale=-1.0)
            recip.append(tile)
        for t in range(PACK):
            scratch = twin[PACK - 1, 1] if t % 2 == 0 else diff[PACK - 1, 0]
            planes = dfn[t][:].rearrange("p (h a c) -> p h a c", h=HALVES, a=2)
            nc.vector.tensor_tensor(
                out=scratch[:].rearrange("p (h c) -> p h c", h=HALVES), in0=planes[:, :, 0, :], in1=planes[:, :, 1, :], op=ALU.min
            )
            pairs = scratch[:].rearrange("p (h b v) -> p h b v", h=HALVES, b=2)
            nc.vector.tensor_tensor(
                out=dfn[t][:, V : 2 * V].rearrange("p (h v) -> p h v", h=HALVES), in0=pairs[:, :, 0, :], in1=pairs[:, :, 1, :], op=ALU.min
            )

        picked = keep.tile([P, PACK, U], F32, name="picked")
        voi = keep.tile([P, PACK, U], F32, name="voi")
        voiced = keep.tile([P, PACK, U], F32, name="voiced")
        hid = keep.tile([P, PACK, U], BF16, name="hid")

        def best(t):
            nc.vector.scalar_tensor_tensor(
                out=dfn[t][:, 0:V],
                in0=dfn[t][:, V : 2 * V],
                scalar=-GAIN,
                in1=recip[t // 2][:, (t % 2) * V : (t % 2 + 1) * V],
                op0=ALU.mult,
                op1=ALU.mult,
            )

        def looked_up(t, notes):
            return dfn[t][:].indirect(note_t[:, notes.start // 16 : notes.stop // 16])

        def voicing(t, notes):
            nc.scalar.activation(out=voi[:, t, notes], in_=picked[:, t, notes], func=ACT.Sigmoid, scale=3.0, bias=1.0)

        def pick_and_voice(t, notes):
            nc.scalar.activation(out=picked[:, t, notes], in_=looked_up(t, notes), func=ACT.Copy)
            voicing(t, notes)

        def amplitude(t, notes):
            nc.vector.scalar_tensor_tensor(
                out=voiced[:, t, notes],
                in0=voi[:, t, notes],
                scalar=unit_t[:, t : t + 1],
                in1=amp_t[:, t, notes],
                op0=ALU.mult,
                op1=ALU.mult,
            )

        def hidden(t, notes):
            nc.vector.scalar_tensor_tensor(
                out=hid[:, t, notes],
                in0=picked[:, t, notes],
                scalar=unit_t[:, t : t + 1],
                in1=voiced[:, t, notes],
                op0=ALU.mult,
                op1=ALU.add,
            )

        w2_grouped = keep.tile([P, N, PACK], BF16, name="w2_grouped", tag="twin30", align_bytes=64)
        nc.vector.tensor_copy(
            out=w2_grouped[:].rearrange("p (c i) j -> p c j i", i=4),
            in_=w2_raw[:].rearrange("p j (c i) -> p c j i", i=4),
        )
        w2_codes = keep.tile([P, N], U32, name="w2_codes", align_bytes=64)
        w2_scales = keep.tile([P, N], U8, name="w2_scales", align_bytes=64)
        nc.vector.quantize_mx(
            out=w2_codes[:].bitcast(FP8X4), scales=w2_scales[:], in_=w2_grouped[:].rearrange("p c j -> p (c j)")
        )

        every = slice(0, U)
        early, late = slice(0, NOTE_HALF), slice(NOTE_HALF, U)
        for t in range(3):
            best(t)
        pick_and_voice(0, every)
        nc.vector.tensor_copy(out=picked[:, 1, :], in_=looked_up(1, every))
        best(3)
        voicing(1, every)
        pick_and_voice(2, every)
        pick_and_voice(3, early)
        pick_and_voice(3, late)
        for steps in (((0, every), (1, every)), ((2, every), (3, early)), ((3, late),)):
            for t, notes in steps:
                amplitude(t, notes)
            for t, notes in steps:
                hidden(t, notes)

        grouped = []
        for h, notes in enumerate((early, late)):
            tile = keep.tile([P, NOTE_HALF, PACK], BF16, name=f"hid_grouped{h}", align_bytes=64)
            dst = tile[:].rearrange("p (c i) t -> p c t i", i=4)
            src = hid[:, :, notes].rearrange("p t (c i) -> p c t i", i=4)
            if h == 0:
                nc.scalar.copy(out=dst, in_=src)
            else:
                nc.vector.tensor_copy(out=dst, in_=src)
            grouped.append(tile)
        for h, notes in ((1, late), (0, early)):
            codes = keep.tile([P, NOTE_HALF], U32, name=f"hid_codes{h}", align_bytes=64)
            scales = keep.tile([P, NOTE_HALF], U8, name=f"hid_scales{h}", align_bytes=64)
            nc.vector.quantize_mx(
                out=codes[:].bitcast(FP8X4), scales=scales[:], in_=grouped[h][:].rearrange("p c t -> p (c t)")
            )
            acc = psum.tile([P, NOTE_HALF], F32, name=f"acc{h}", tag=f"bank{h}0")
            nc.tensor.matmul_mx(
                out=acc[:],
                lhsT=w2_codes[:].bitcast(FP8X4),
                lhsT_scale=w2_scales[:],
                rhs=codes[:].bitcast(FP8X4),
                rhs_scale=scales[:],
                start=True,
                stop=True,
            )
            result = keep.tile([P, NOTE_HALF], F32, name=f"result{h}")
            if h == 1:
                nc.scalar.copy(out=result[:], in_=acc[:])
                nc.scalar.dma_start(out=out[:, notes], in_=result[:])
            else:
                nc.vector.tensor_copy(out=result[:], in_=acc[:])
                nc.sync.dma_start(out=out[:, notes], in_=result[:])
